import numpy as np, ml_dtypes
CORES = [24,40,56,80,88,96]
N = 6
PG, W, NP = 32, 64, 32
def entries(a): return a.T.reshape(-1)
def pack(v, P): return np.ascontiguousarray(np.asarray(v, np.int32).reshape(-1, P).T)
def lists(rng, how):
    I = rng.integers(0, N * PG, (N, NP))
    if how == "alike": I[:] = rng.integers(0, N * PG, (N, 1))
    if how == "hotrank": I = PG * int(rng.integers(N)) + rng.integers(0, PG, (N, NP))
    if how == "own": I = PG * np.arange(N).reshape(N, 1) + rng.integers(0, PG, (N, NP))
    if how == "edge": I = PG * rng.integers(0, N, (N, NP)) + np.where(rng.random((N, NP)) < 0.5, 0, PG - 1)
    if how == "swap": s = int(rng.integers(1, N)); I = np.stack([PG * ((r + s) % N) + np.concatenate([rng.permutation(PG), rng.integers(0, PG, NP)])[:NP] for r in range(N)])
    return {"pt": np.stack([pack(I[r], 16) for r in range(N)])}
def setup_inputs(rng):
    return dict({"pool": rng.standard_normal((N, PG * 128, W), dtype=np.float32).astype(ml_dtypes.bfloat16)}, **lists(rng, "uniform"))
def setup_inputs_alike(rng):
    d = setup_inputs(rng); d.update(lists(rng, "alike"))
    for k in ("pool",): d[k] = (d[k].astype(np.float32) * 1048576.0).astype(d[k].dtype)
    return d
def setup_inputs_edge(rng):
    d = setup_inputs(rng); d.update(lists(rng, "edge"))
    for k in ("pool",): d[k] = (d[k].astype(np.float32) * (1 / 1024.0)).astype(d[k].dtype)
    return d
def setup_inputs_hotrank(rng):
    d = setup_inputs(rng); d.update(lists(rng, "hotrank"))
    return d
def setup_inputs_own(rng):
    d = setup_inputs(rng); d.update(lists(rng, "own"))
    return d
def setup_inputs_swap(rng):
    d = setup_inputs(rng); d.update(lists(rng, "swap"))
    return d
def check_inputs(x):
    bad = []
    if x["pt"].min() < 0 or x["pt"].max() >= N * PG: bad.append("pt out of range")
    return bad
def reference(pool, pt):
    A = np.concatenate(list(pool), axis=0).reshape(N * PG, 128, W)
    return {"y": np.stack([A[entries(pt[r])].reshape(NP * 128, W) for r in range(N)])}

@@ -1,0 +1,267 @@
+from concourse.bass import DstId, RemoteDMATransfer
+from concourse.mybir import AluOpType, ActivationFunctionType
+
+N = 6
+K = 8
+SW = 2048 // K
+NB = SW // 128
+WW = N * 128
+SIM_CORES = 112
+
+SCRATCH = {
+    "S": ("sbuf", [128, 2048], "bfloat16"),
+    "Y": ("sbuf", [128, 2048], "bfloat16"),
+    "pt32": ("sbuf", [128, 2], "int32"),
+    "ptf": ("sbuf", [128, 2], "float32"),
+    "mi": ("sbuf", [128, 4], "int32"),
+    "mi2": ("sbuf", [128, 4], "int32"),
+    "msk": ("sbuf", [128, 4], "float32"),
+    "li": ("sbuf", [128, 128], "int32"),
+    "li2": ("sbuf", [128, 128], "int32"),
+    "lm": ("sbuf", [128, 128], "bfloat16"),
+    "rr": ("sbuf", [128, 8], "bfloat16"),
+    "LB": ("sbuf", [128, 8], "bfloat16"),
+    "pq": ("psum", [128, 512], "float32"),
+    "H": ("sbuf", [128, 2 * SW], "bfloat16"),
+    "HL": ("sbuf", [128, 8], "bfloat16"),
+    "A": ("sbuf", [128, N * SW], "bfloat16"),
+    "AL": ("sbuf", [128, N * 8], "bfloat16"),
+    "ones": ("sbuf", [128, 128], "bfloat16"),
+    "ident": ("sbuf", [128, 128], "bfloat16"),
+    "qi": ("sbuf", [128, 1], "int32"),
+    "qi2": ("sbuf", [128, 1], "int32"),
+    "qc": ("sbuf", [128, 1], "float32"),
+    "qc2": ("sbuf", [128, 1], "float32"),
+    "OFF": ("sbuf", [128, N * 16], "uint16"),
+    "W": ("sbuf", [128, NB * WW], "bfloat16"),
+    "O": ("sbuf", [128, N * SW], "bfloat16"),
+    "Z": ("sbuf", [128, N * SW], "bfloat16"),
+}
+for _s in range(N):
+    SCRATCH["ps%d" % _s] = ("psum", [128, 1024], "bfloat16")
+
+SEMAPHORES = ["s_pt", "s_pool", "c_io", "c_a", "c_b", "c_r", "c_m", "c_l", "sent", "yarr", "done",
+              "hl", "hd", "k_one", "k_id", "k_q", "k_q2", "k_qc", "evv", "evs"]
+for _s in range(N):
+    SEMAPHORES += ["la%d" % _s, "da%d" % _s, "of%d" % _s, "tf%d" % _s, "ga%d" % _s, "tb%d" % _s, "z%d" % _s]
+
+
+def _plan(T, topo):
+    ranks = list(T.cores)
+    rchips = [topo.chip(c) for c in ranks]
+    by_chip = {}
+    for c in range(SIM_CORES):
+        by_chip.setdefault(topo.chip(c), []).append(c)
+
+    def near(x):
+        return sum(1 for rc in rchips if topo.same_plane(x, rc) or topo.mates(x, rc))
+
+    free = sorted([x for x in by_chip if x not in rchips], key=lambda x: (-near(x), x))
+    per_die = {}
+    for x in free[:K // 2]:
+        seen = []
+        for c in by_chip[x]:
+            if topo.die(c) not in seen and all(topo.may_write(c, r) for r in ranks):
+                seen.append(topo.die(c))
+                per_die.setdefault(topo.die(c), []).append(c)
+    dies = sorted(per_die, reverse=True)
+    middle = []
+    for d in dies:
+        middle += per_die[d]
+    helpers = {}
+    for r, rc in enumerate(ranks):
+        hs = []
+        for d in dies:
+            can = [c for c in by_chip[topo.chip(rc)]
+                   if c != rc and topo.die(c) == d and all(topo.may_write(c, m) for m in middle)]
+            first = [k for k in range(0, K, 2) if topo.die(middle[k]) == d]
+            for j, k in enumerate(first):
+                hs.append((can[j], k))
+        helpers[r] = hs
+    return ranks, middle, helpers
+
+
+def _bits(mask):
+    return [b for b in range(16) if (mask >> b) & 1]
+
+
+def _part(mask, parts, i):
+    b = _bits(mask)
+    n = len(b) // parts
+    return sum(1 << e for e in b[i * n:(i + 1) * n]), n
+
+
+def _dst(topo, c):
+    rid, pid, _ = topo.addr(c)
+    return DstId(rid=rid, pnc=pid)
+
+
+def _rank(g, core, r, T, topo, helpers):
+    sem = T.sem
+    v, pe = g.vector, g.tensor
+    hs = helpers[r]
+    nh = len(hs)
+    g.scalar.dma_start(T.pt32[0:16, 0:2], T.pt[:]).then_inc(sem.s_pt, 16)
+    g.sync.dma_start(T.S[:], T.pool[:]).then_inc(sem.s_pool, 16)
+    g.iota(T.mi[0:16, 0:4], [[-4, 4]], 0, 1).then_inc(sem.c_io, 1)
+    g.iota(T.li[0:16, :], [[0, 8], [-1, 4], [0, 4]], 4, 1).then_inc(sem.c_io, 1)
+    v.wait_ge(sem.c_io, 2)
+    v.tensor_scalar(T.mi2[0:16, :], T.mi[0:16, :], 2, None, AluOpType.arith_shift_right).then_inc(sem.c_a, 1)
+    v.tensor_scalar(T.li2[0:16, :], T.li[0:16, :], 3, None, AluOpType.bitwise_and).then_inc(sem.c_a, 1)
+    v.wait_ge(sem.c_a, 2)
+    v.tensor_scalar(T.msk[0:16, :], T.mi2[0:16, :], 0, None, AluOpType.is_equal).then_inc(sem.c_b, 1)
+    v.tensor_scalar(T.lm[0:16, :], T.li2[0:16, :], 0, None, AluOpType.is_equal).then_inc(sem.c_b, 1)
+    v.wait_ge(sem.s_pt, 16)
+    v.tensor_copy(T.ptf[0:16, :], T.pt32[0:16, :]).then_inc(sem.c_b, 1)
+    v.wait_ge(sem.c_b, 3)
+    for n in range(2):
+        v.tensor_scalar(T.rr[0:16, 4 * n:4 * n + 4], T.msk[0:16, :], T.ptf[0:16, n:n + 1], None,
+                        AluOpType.mult).then_inc(sem.c_r, 1)
+    pe.wait_ge(sem.c_b, 3)
+    pe.wait_ge(sem.c_r, 2)
+    pe.matmul(T.pq[:, 0:8], T.lm[0:16, :], T.rr[0:16, :], True, True).then_inc(sem.c_m, 1)
+    v.wait_ge(sem.c_m, 1)
+    v.tensor_copy(T.LB[:], T.pq[:, 0:8]).then_inc(sem.c_l, 1)
+    g.wait_ge(sem.c_l, 1)
+    sent = 0
+    tl, td = [], []
+    for i, (h, k) in enumerate(hs):
+        m, n = _part(topo.mask(core, h), nh, i)
+        tl.append(RemoteDMATransfer(dst_ids=[_dst(topo, h)], dma_engine_mask=m, remote_sem=sem.hl,
+                                    src=T.LB[:], dst=T.HL[:]))
+        td.append(RemoteDMATransfer(dst_ids=[_dst(topo, h)], dma_engine_mask=m, remote_sem=sem.hd,
+                                    src=T.S[:, k * SW:(k + 2) * SW], dst=T.H[:]))
+        sent += 2 * n
+    g.remote_dma_fused(tl, local_sem=sem.sent)
+    g.wait_ge(sem.s_pool, 16)
+    g.remote_dma_fused(td, local_sem=sem.sent)
+    g.wait_ge(sem.sent, sent)
+    g.sync.wait_ge(sem.yarr, K * len(_bits(_off_mask(T, topo, core))))
+    g.sync.dma_start(T.y[:], T.Y[:]).then_inc(sem.done, 16)
+    g.sync.wait_ge(sem.done, 16)
+
+
+def _off_mask(T, topo, core):
+    _, middle, _ = _plan(T, topo)
+    return topo.mask(middle[0], core)
+
+
+def _helper(g, core, r, k, T, topo, ranks, middle, nh):
+    sem = T.sem
+    _, n_in = _part(topo.mask(ranks[r], core), nh, 0)
+    tl, td = [], []
+    sent = 0
+    for j in range(2):
+        d = middle[k + j]
+        m, n = _part(topo.mask(core, d), 2, j)
+        tl.append(RemoteDMATransfer(dst_ids=[_dst(topo, d)], dma_engine_mask=m, remote_sem=sem["la%d" % r],
+                                    src=T.HL[:], dst=T.AL[:, r * 8:(r + 1) * 8]))
+        td.append(RemoteDMATransfer(dst_ids=[_dst(topo, d)], dma_engine_mask=m, remote_sem=sem["da%d" % r],
+                                    src=T.H[:, j * SW:(j + 1) * SW], dst=T.A[:, r * SW:(r + 1) * SW]))
+        sent += 2 * n
+    g.wait_ge(sem.hl, n_in)
+    g.remote_dma_fused(tl, local_sem=sem.sent)
+    g.wait_ge(sem.hd, n_in)
+    g.remote_dma_fused(td, local_sem=sem.sent)
+    g.wait_ge(sem.sent, sent)
+
+
+def _middle(g, core, k, T, topo, ranks):
+    sem = T.sem
+    v, sc, pe = g.vector, g.scalar, g.tensor
+    n_in = len(_bits(topo.mask(ranks[0], core))) // 2
+    x = topo.chip(core)
+
+    def far(r):
+        rc = topo.chip(ranks[r])
+        return 0 if (topo.same_plane(x, rc) or topo.mates(x, rc)) else 1
+
+    order = sorted(range(N), key=lambda r: (far(r), r))
+    on_v = {r: (i % 2 == 0) for i, r in enumerate(order)}
+
+    def copy(r, out, in_):
+        if on_v[r]:
+            return v.tensor_copy(out, in_)
+        return sc.activation(out, in_, ActivationFunctionType.Copy)
+
+    def q_of(r):
+        return v if on_v[r] else sc
+
+    v.memset(T.ones[:], 1.0).then_inc(sem.k_one, 1)
+    g.iota(T.qi[:], [[0, 1]], 0, 1).then_inc(sem.k_q, 1)
+    g.wait_ge(sem.k_one, 1)
+    g.affine_select(T.ident[:], T.ones[:], [[-1, 128]], AluOpType.is_equal, 0.0, 0, 1).then_inc(sem.k_id, 1)
+    v.wait_ge(sem.k_q, 1)
+    v.tensor_scalar(T.qi2[:], T.qi[:], 3, None, AluOpType.bitwise_and).then_inc(sem.k_q2, 1)
+    v.wait_ge(sem.k_q2, 1)
+    v.tensor_copy(T.qc[:], T.qi2[:]).then_inc(sem.k_qc, 1)
+    v.tensor_scalar(T.qc2[:], T.qi2[:], float(WW), None, AluOpType.add).then_inc(sem.k_qc, 1)
+    v.wait_ge(sem.k_qc, 2)
+    for r in order:
+        v.wait_ge(sem["la%d" % r], n_in)
+        for b, col in enumerate((T.qc, T.qc2)):
+            v.tensor_scalar(T.OFF[:, r * 16 + 8 * b:r * 16 + 8 * b + 8], T.AL[:, r * 8:(r + 1) * 8], 4.0, col[:],
+                            AluOpType.mult, AluOpType.add).then_inc(sem["of%d" % r], 1)
+    pe.wait_ge(sem.k_id, 1)
+    nev = {True: 0, False: 0}
+    for s in order:
+        ps = T["ps%d" % s]
+        pe.wait_ge(sem["da%d" % s], n_in)
+        for b in range(NB):
+            pe.transpose(ps[:, b * 128:(b + 1) * 128], T.A[:, s * SW + b * 128:s * SW + (b + 1) * 128],
+                         T.ident[:]).then_inc(sem["tf%d" % s], 1)
+        q_of(s).wait_ge(sem["tf%d" % s], NB)
+        for b in range(NB):
+            copy(s, T.W[:, b * WW + s * 128:b * WW + (s + 1) * 128],
+                 ps[:, b * 128:(b + 1) * 128]).then_inc(sem.evv if on_v[s] else sem.evs, 1)
+            nev[on_v[s]] += 1
+    for q in (v, sc):
+        q.wait_ge(sem.evv, nev[True])
+        q.wait_ge(sem.evs, nev[False])
+
+    def gather(r):
+        q_of(r).wait_ge(sem["of%d" % r], 2)
+        copy(r, T.O[:, r * SW:(r + 1) * SW],
+             T.W[:, 0:NB * WW].indirect(T.OFF[:, r * 16:(r + 1) * 16])).then_inc(sem["ga%d" % r], 1)
+
+    def back(r):
+        q_of(r).wait_ge(sem["tb%d" % r], NB)
+        copy(r, T.Z[:, r * SW:(r + 1) * SW], T["ps%d" % r][:, 0:SW]).then_inc(sem["z%d" % r], 1)
+
+    askers = sorted(range(N), key=lambda r: (-far(r), order.index(r)))
+    askers = [r for pair in zip([r for r in askers if on_v[r]], [r for r in askers if not on_v[r]]) for r in pair]
+    for flag in (True, False):
+        mine = [r for r in askers if on_v[r] == flag]
+        gather(mine[0])
+        for i in range(1, len(mine)):
+            gather(mine[i])
+            back(mine[i - 1])
+        back(mine[-1])
+    sent = 0
+    for r in askers:
+        pe.wait_ge(sem["ga%d" % r], 1)
+        for b in range(NB):
+            pe.transpose(T["ps%d" % r][:, b * 128:(b + 1) * 128],
+                         T.O[:, r * SW + b * 128:r * SW + (b + 1) * 128], T.ident[:]).then_inc(sem["tb%d" % r], 1)
+        rid, pid, _ = topo.addr(ranks[r])
+        m = topo.mask(core, ranks[r])
+        g.wait_ge(sem["z%d" % r], 1)
+        g.remote_dma(T.Y[:, k * SW:(k + 1) * SW], T.Z[:, r * SW:(r + 1) * SW], sem.yarr, sem.sent, pid, rid, m)
+        sent += len(_bits(m))
+    g.wait_ge(sem.sent, sent)
+
+
+def rank_program(g, core, T, topo):
+    ranks, middle, helpers = _plan(T, topo)
+    r = T.rank_of(core)
+    if r is not None:
+        _rank(g, core, r, T, topo, helpers)
+        return
+    if core in middle:
+        _middle(g, core, middle.index(core), T, topo, ranks)
+        return
+    for rr, hs in helpers.items():
+        for h, k in hs:
+            if h == core:
+                _helper(g, core, rr, k, T, topo, ranks, middle, len(hs))
+                return

@@ -3,9 +3,9 @@ from concourse.mybir import AluOpType, ActivationFunctionType
 
 N = 6
 K = 8
+G = 2
 SW = 2048 // K
 NB = SW // 128
-WW = N * 128
 SIM_CORES = 112
 
 SCRATCH = {
@@ -23,17 +23,17 @@ SCRATCH = {
     "LB": ("sbuf", [128, 8], "bfloat16"),
     "pq": ("psum", [128, 512], "float32"),
     "H": ("sbuf", [128, 2 * SW], "bfloat16"),
+    "HT": ("sbuf", [128, 2 * SW], "bfloat16"),
     "HL": ("sbuf", [128, 8], "bfloat16"),
-    "A": ("sbuf", [128, N * SW], "bfloat16"),
-    "AL": ("sbuf", [128, N * 8], "bfloat16"),
     "ones": ("sbuf", [128, 128], "bfloat16"),
     "ident": ("sbuf", [128, 128], "bfloat16"),
+    "AL": ("sbuf", [128, N * 8], "bfloat16"),
     "qi": ("sbuf", [128, 1], "int32"),
     "qi2": ("sbuf", [128, 1], "int32"),
     "qc": ("sbuf", [128, 1], "float32"),
     "qc2": ("sbuf", [128, 1], "float32"),
     "OFF": ("sbuf", [128, N * 16], "uint16"),
-    "W": ("sbuf", [128, NB * WW], "bfloat16"),
+    "W": ("sbuf", [128, N * SW], "bfloat16"),
     "O": ("sbuf", [128, N * SW], "bfloat16"),
     "Z": ("sbuf", [128, N * SW], "bfloat16"),
 }
@@ -41,7 +41,7 @@ for _s in range(N):
     SCRATCH["ps%d" % _s] = ("psum", [128, 1024], "bfloat16")
 
 SEMAPHORES = ["s_pt", "s_pool", "c_io", "c_a", "c_b", "c_r", "c_m", "c_l", "sent", "yarr", "done",
-              "hl", "hd", "k_one", "k_id", "k_q", "k_q2", "k_qc", "evv", "evs"]
+              "hl", "hd", "k_one", "k_id", "k_q", "k_q2", "k_qc", "evv"]
 for _s in range(N):
     SEMAPHORES += ["la%d" % _s, "da%d" % _s, "of%d" % _s, "tf%d" % _s, "ga%d" % _s, "tb%d" % _s, "z%d" % _s]
 
@@ -53,32 +53,37 @@ def _plan(T, topo):
     for c in range(SIM_CORES):
         by_chip.setdefault(topo.chip(c), []).append(c)
 
-    def near(x):
-        return sum(1 for rc in rchips if topo.same_plane(x, rc) or topo.mates(x, rc))
+    def one_hop(x, rc):
+        return topo.same_plane(x, rc) or topo.mates(x, rc)
 
-    free = sorted([x for x in by_chip if x not in rchips], key=lambda x: (-near(x), x))
-    per_die = {}
-    for x in free[:K // 2]:
-        seen = []
-        for c in by_chip[x]:
-            if topo.die(c) not in seen and all(topo.may_write(c, r) for r in ranks):
-                seen.append(topo.die(c))
-                per_die.setdefault(topo.die(c), []).append(c)
-    dies = sorted(per_die, reverse=True)
-    middle = []
-    for d in dies:
-        middle += per_die[d]
+    free = sorted([x for x in by_chip if x not in rchips],
+                  key=lambda x: (-sum(1 for rc in rchips if one_hop(x, rc)), x))
+    nch = K // 2
+    middle, dies = [], []
+    for gi in range(G):
+        per_die = {}
+        for x in free[gi * nch:(gi + 1) * nch]:
+            seen = []
+            for c in by_chip[x]:
+                if topo.die(c) not in seen and all(topo.may_write(c, r) for r in ranks):
+                    seen.append(topo.die(c))
+                    per_die.setdefault(topo.die(c), []).append(c)
+        dies = sorted(per_die, reverse=True)
+        middle.append([c for d in dies for c in per_die[d]])
+    pref = sorted(range(N), key=lambda r: (-sum(1 for x in free[:nch] if one_hop(x, rchips[r])), r))
+    groups = [sorted(pref[gi * (N // G):(gi + 1) * (N // G)]) for gi in range(G)]
+    every = [c for ms in middle for c in ms]
     helpers = {}
     for r, rc in enumerate(ranks):
         hs = []
         for d in dies:
             can = [c for c in by_chip[topo.chip(rc)]
-                   if c != rc and topo.die(c) == d and all(topo.may_write(c, m) for m in middle)]
-            first = [k for k in range(0, K, 2) if topo.die(middle[k]) == d]
+                   if c != rc and topo.die(c) == d and all(topo.may_write(c, m) for m in every)]
+            first = [k for k in range(0, K, 2) if topo.die(middle[0][k]) == d]
             for j, k in enumerate(first):
                 hs.append((can[j], k))
         helpers[r] = hs
-    return ranks, middle, helpers
+    return ranks, middle, groups, helpers
 
 
 def _bits(mask):
@@ -96,7 +101,13 @@ def _dst(topo, c):
     return DstId(rid=rid, pnc=pid)
 
 
-def _rank(g, core, r, T, topo, helpers):
+def _identity(g, T):
+    g.vector.memset(T.ones[:], 1.0).then_inc(T.sem.k_one, 1)
+    g.wait_ge(T.sem.k_one, 1)
+    g.affine_select(T.ident[:], T.ones[:], [[-1, 128]], AluOpType.is_equal, 0.0, 0, 1).then_inc(T.sem.k_id, 1)
+
+
+def _rank(g, core, r, T, topo, mine, helpers):
     sem = T.sem
     v, pe = g.vector, g.tensor
     hs = helpers[r]
@@ -136,113 +147,88 @@ def _rank(g, core, r, T, topo, helpers):
     g.wait_ge(sem.s_pool, 16)
     g.remote_dma_fused(td, local_sem=sem.sent)
     g.wait_ge(sem.sent, sent)
-    g.sync.wait_ge(sem.yarr, K * len(_bits(_off_mask(T, topo, core))))
+    g.sync.wait_ge(sem.yarr, sum(len(_bits(topo.mask(m, core))) for m in mine))
     g.sync.dma_start(T.y[:], T.Y[:]).then_inc(sem.done, 16)
     g.sync.wait_ge(sem.done, 16)
 
 
-def _off_mask(T, topo, core):
-    _, middle, _ = _plan(T, topo)
-    return topo.mask(middle[0], core)
-
-
-def _helper(g, core, r, k, T, topo, ranks, middle, nh):
+def _helper(g, core, r, k, T, topo, ranks, middle, gr, nh):
     sem = T.sem
+    v, pe = g.vector, g.tensor
     _, n_in = _part(topo.mask(ranks[r], core), nh, 0)
+    _identity(g, T)
     tl, td = [], []
     sent = 0
     for j in range(2):
-        d = middle[k + j]
+        d = middle[gr][k + j]
         m, n = _part(topo.mask(core, d), 2, j)
         tl.append(RemoteDMATransfer(dst_ids=[_dst(topo, d)], dma_engine_mask=m, remote_sem=sem["la%d" % r],
                                     src=T.HL[:], dst=T.AL[:, r * 8:(r + 1) * 8]))
-        td.append(RemoteDMATransfer(dst_ids=[_dst(topo, d)], dma_engine_mask=m, remote_sem=sem["da%d" % r],
-                                    src=T.H[:, j * SW:(j + 1) * SW], dst=T.A[:, r * SW:(r + 1) * SW]))
-        sent += 2 * n
+        sent += n
+        for gi in range(G):
+            d = middle[gi][k + j]
+            m, n = _part(topo.mask(core, d), 2 * G, j * G + gi)
+            td.append(RemoteDMATransfer(dst_ids=[_dst(topo, d)], dma_engine_mask=m, remote_sem=sem["da%d" % r],
+                                        src=T.HT[:, j * SW:(j + 1) * SW], dst=T.W[:, r * SW:(r + 1) * SW]))
+            sent += n
     g.wait_ge(sem.hl, n_in)
     g.remote_dma_fused(tl, local_sem=sem.sent)
-    g.wait_ge(sem.hd, n_in)
+    pe.wait_ge(sem.k_id, 1)
+    pe.wait_ge(sem.hd, n_in)
+    for j in range(2):
+        ps = T["ps%d" % j]
+        for b in range(NB):
+            pe.transpose(ps[:, b * 128:(b + 1) * 128], T.H[:, j * SW + b * 128:j * SW + (b + 1) * 128],
+                         T.ident[:]).then_inc(sem["tf%d" % j], 1)
+        v.wait_ge(sem["tf%d" % j], NB)
+        for b in range(NB):
+            v.tensor_copy(T.HT[:, j * SW + b:(j + 1) * SW:NB], ps[:, b * 128:(b + 1) * 128]).then_inc(sem.evv, 1)
+    g.wait_ge(sem.evv, 2 * NB)
     g.remote_dma_fused(td, local_sem=sem.sent)
     g.wait_ge(sem.sent, sent)
 
 
-def _middle(g, core, k, T, topo, ranks):
+def _middle(g, core, k, T, topo, ranks, askers):
     sem = T.sem
     v, sc, pe = g.vector, g.scalar, g.tensor
-    n_in = len(_bits(topo.mask(ranks[0], core))) // 2
-    x = topo.chip(core)
+    off = len(_bits(topo.mask(ranks[0], core)))
+    n_list, n_data = off // 2, off // (2 * G)
+    na = len(askers)
+    askers = [askers[(k + t) % na] for t in range(na)]
 
-    def far(r):
-        rc = topo.chip(ranks[r])
-        return 0 if (topo.same_plane(x, rc) or topo.mates(x, rc)) else 1
-
-    order = sorted(range(N), key=lambda r: (far(r), r))
-    on_v = {r: (i % 2 == 0) for i, r in enumerate(order)}
-
-    def copy(r, out, in_):
-        if on_v[r]:
-            return v.tensor_copy(out, in_)
-        return sc.activation(out, in_, ActivationFunctionType.Copy)
-
-    def q_of(r):
-        return v if on_v[r] else sc
-
-    v.memset(T.ones[:], 1.0).then_inc(sem.k_one, 1)
     g.iota(T.qi[:], [[0, 1]], 0, 1).then_inc(sem.k_q, 1)
-    g.wait_ge(sem.k_one, 1)
-    g.affine_select(T.ident[:], T.ones[:], [[-1, 128]], AluOpType.is_equal, 0.0, 0, 1).then_inc(sem.k_id, 1)
+    _identity(g, T)
     v.wait_ge(sem.k_q, 1)
     v.tensor_scalar(T.qi2[:], T.qi[:], 3, None, AluOpType.bitwise_and).then_inc(sem.k_q2, 1)
     v.wait_ge(sem.k_q2, 1)
-    v.tensor_copy(T.qc[:], T.qi2[:]).then_inc(sem.k_qc, 1)
-    v.tensor_scalar(T.qc2[:], T.qi2[:], float(WW), None, AluOpType.add).then_inc(sem.k_qc, 1)
+    v.tensor_scalar(T.qc[:], T.qi2[:], 2.0, None, AluOpType.mult).then_inc(sem.k_qc, 1)
+    v.tensor_scalar(T.qc2[:], T.qi2[:], 2.0, 1.0, AluOpType.mult, AluOpType.add).then_inc(sem.k_qc, 1)
     v.wait_ge(sem.k_qc, 2)
-    for r in order:
-        v.wait_ge(sem["la%d" % r], n_in)
-        for b, col in enumerate((T.qc, T.qc2)):
-            v.tensor_scalar(T.OFF[:, r * 16 + 8 * b:r * 16 + 8 * b + 8], T.AL[:, r * 8:(r + 1) * 8], 4.0, col[:],
-                            AluOpType.mult, AluOpType.add).then_inc(sem["of%d" % r], 1)
-    pe.wait_ge(sem.k_id, 1)
-    nev = {True: 0, False: 0}
-    for s in order:
-        ps = T["ps%d" % s]
-        pe.wait_ge(sem["da%d" % s], n_in)
-        for b in range(NB):
-            pe.transpose(ps[:, b * 128:(b + 1) * 128], T.A[:, s * SW + b * 128:s * SW + (b + 1) * 128],
-                         T.ident[:]).then_inc(sem["tf%d" % s], 1)
-        q_of(s).wait_ge(sem["tf%d" % s], NB)
-        for b in range(NB):
-            copy(s, T.W[:, b * WW + s * 128:b * WW + (s + 1) * 128],
-                 ps[:, b * 128:(b + 1) * 128]).then_inc(sem.evv if on_v[s] else sem.evs, 1)
-            nev[on_v[s]] += 1
-    for q in (v, sc):
-        q.wait_ge(sem.evv, nev[True])
-        q.wait_ge(sem.evs, nev[False])
-
-    def gather(r):
-        q_of(r).wait_ge(sem["of%d" % r], 2)
-        copy(r, T.O[:, r * SW:(r + 1) * SW],
-             T.W[:, 0:NB * WW].indirect(T.OFF[:, r * 16:(r + 1) * 16])).then_inc(sem["ga%d" % r], 1)
-
-    def back(r):
-        q_of(r).wait_ge(sem["tb%d" % r], NB)
-        copy(r, T.Z[:, r * SW:(r + 1) * SW], T["ps%d" % r][:, 0:SW]).then_inc(sem["z%d" % r], 1)
-
-    askers = sorted(range(N), key=lambda r: (-far(r), order.index(r)))
-    askers = [r for pair in zip([r for r in askers if on_v[r]], [r for r in askers if not on_v[r]]) for r in pair]
-    for flag in (True, False):
-        mine = [r for r in askers if on_v[r] == flag]
-        gather(mine[0])
-        for i in range(1, len(mine)):
-            gather(mine[i])
-            back(mine[i - 1])
-        back(mine[-1])
-    sent = 0
     for r in askers:
+        v.wait_ge(sem["la%d" % r], n_list)
+        for b, col in enumerate((T.qc, T.qc2)):
+            v.tensor_scalar(T.OFF[:, r * 16 + 8 * b:r * 16 + 8 * b + 8], T.AL[:, r * 8:(r + 1) * 8], 8.0, col[:],
+                            AluOpType.mult, AluOpType.add).then_inc(sem["of%d" % r], 1)
+    for q in (v, sc):
+        for s in range(N):
+            q.wait_ge(sem["da%d" % s], n_data)
+    pe.wait_ge(sem.k_id, 1)
+    sent = 0
+    for i, r in enumerate(askers):
+        ps = T["ps%d" % r]
+        win = T.W[:].indirect(T.OFF[:, r * 16:(r + 1) * 16])
+        if i == 0:
+            v.wait_ge(sem["of%d" % r], 2)
+            v.tensor_copy(T.O[:, r * SW:(r + 1) * SW], win).then_inc(sem["ga%d" % r], 1)
+        else:
+            sc.wait_ge(sem["of%d" % r], 2)
+            sc.activation(T.O[:, r * SW:(r + 1) * SW], win, ActivationFunctionType.Copy).then_inc(sem["ga%d" % r], 1)
         pe.wait_ge(sem["ga%d" % r], 1)
         for b in range(NB):
-            pe.transpose(T["ps%d" % r][:, b * 128:(b + 1) * 128],
+            pe.transpose(ps[:, b * 128:(b + 1) * 128],
                          T.O[:, r * SW + b * 128:r * SW + (b + 1) * 128], T.ident[:]).then_inc(sem["tb%d" % r], 1)
+        v.wait_ge(sem["tb%d" % r], NB)
+        v.tensor_copy(T.Z[:, r * SW:(r + 1) * SW], ps[:, 0:SW]).then_inc(sem["z%d" % r], 1)
         rid, pid, _ = topo.addr(ranks[r])
         m = topo.mask(core, ranks[r])
         g.wait_ge(sem["z%d" % r], 1)
@@ -252,16 +238,18 @@ def _middle(g, core, k, T, topo, ranks):
 
 
 def rank_program(g, core, T, topo):
-    ranks, middle, helpers = _plan(T, topo)
+    ranks, middle, groups, helpers = _plan(T, topo)
+    group_of = {r: gi for gi, rs in enumerate(groups) for r in rs}
     r = T.rank_of(core)
     if r is not None:
-        _rank(g, core, r, T, topo, helpers)
+        _rank(g, core, r, T, topo, middle[group_of[r]], helpers)
         return
-    if core in middle:
-        _middle(g, core, middle.index(core), T, topo, ranks)
-        return
+    for gi in range(G):
+        if core in middle[gi]:
+            _middle(g, core, middle[gi].index(core), T, topo, ranks, groups[gi])
+            return
     for rr, hs in helpers.items():
         for h, k in hs:
             if h == core:
-                _helper(g, core, rr, k, T, topo, ranks, middle, len(hs))
+                _helper(g, core, rr, k, T, topo, ranks, middle, group_of[rr], len(hs))
                 return

@@ -12,6 +12,7 @@ SCRATCH = {
     "S": ("sbuf", [128, 2048], "bfloat16"),
     "Y": ("sbuf", [128, 2048], "bfloat16"),
     "pt32": ("sbuf", [128, 2], "int32"),
+    "HP": ("sbuf", [128, 2], "int32"),
     "ptf": ("sbuf", [128, 2], "float32"),
     "mi": ("sbuf", [128, 4], "int32"),
     "mi2": ("sbuf", [128, 4], "int32"),
@@ -20,18 +21,16 @@ SCRATCH = {
     "li2": ("sbuf", [128, 128], "int32"),
     "lm": ("sbuf", [128, 128], "bfloat16"),
     "rr": ("sbuf", [128, 8], "bfloat16"),
-    "LB": ("sbuf", [128, 8], "bfloat16"),
-    "pq": ("psum", [128, 512], "float32"),
-    "H": ("sbuf", [128, 2 * SW], "bfloat16"),
-    "HT": ("sbuf", [128, 2 * SW], "bfloat16"),
-    "HL": ("sbuf", [128, 8], "bfloat16"),
-    "ones": ("sbuf", [128, 128], "bfloat16"),
-    "ident": ("sbuf", [128, 128], "bfloat16"),
-    "AL": ("sbuf", [128, N * 8], "bfloat16"),
     "qi": ("sbuf", [128, 1], "int32"),
     "qi2": ("sbuf", [128, 1], "int32"),
     "qc": ("sbuf", [128, 1], "float32"),
     "qc2": ("sbuf", [128, 1], "float32"),
+    "OH": ("sbuf", [128, 16], "uint16"),
+    "pq": ("psum", [128, 512], "float32"),
+    "H": ("sbuf", [128, 2 * SW], "bfloat16"),
+    "HT": ("sbuf", [128, 2 * SW], "bfloat16"),
+    "ones": ("sbuf", [128, 128], "bfloat16"),
+    "ident": ("sbuf", [128, 128], "bfloat16"),
     "OFF": ("sbuf", [128, N * 16], "uint16"),
     "W": ("sbuf", [128, N * SW], "bfloat16"),
     "O": ("sbuf", [128, N * SW], "bfloat16"),
@@ -41,9 +40,9 @@ for _s in range(N):
     SCRATCH["ps%d" % _s] = ("psum", [128, 1024], "bfloat16")
 
 SEMAPHORES = ["s_pt", "s_pool", "c_io", "c_a", "c_b", "c_r", "c_m", "c_l", "sent", "yarr", "done",
-              "hl", "hd", "k_one", "k_id", "k_q", "k_q2", "k_qc", "evv"]
+              "hl", "hd0", "hd1", "k_one", "k_id", "k_q", "k_q2", "k_qc"]
 for _s in range(N):
-    SEMAPHORES += ["la%d" % _s, "da%d" % _s, "of%d" % _s, "tf%d" % _s, "ga%d" % _s, "tb%d" % _s, "z%d" % _s]
+    SEMAPHORES += ["la%d" % _s, "da%d" % _s, "tf%d" % _s, "ga%d" % _s, "tb%d" % _s, "z%d" % _s]
 
 
 def _plan(T, topo):
@@ -96,6 +95,12 @@ def _part(mask, parts, i):
     return sum(1 << e for e in b[i * n:(i + 1) * n]), n
 
 
+def _lane(mask, lane, parts, i):
+    b = _bits(mask)[lane::2]
+    n = len(b) // parts
+    return sum(1 << e for e in b[i * n:(i + 1) * n]), n
+
+
 def _dst(topo, c):
     rid, pid, _ = topo.addr(c)
     return DstId(rid=rid, pnc=pid)
@@ -107,23 +112,26 @@ def _identity(g, T):
     g.affine_select(T.ident[:], T.ones[:], [[-1, 128]], AluOpType.is_equal, 0.0, 0, 1).then_inc(T.sem.k_id, 1)
 
 
-def _rank(g, core, r, T, topo, mine, helpers):
+def _make_offsets(g, T, ptile, arrived, count):
     sem = T.sem
     v, pe = g.vector, g.tensor
-    hs = helpers[r]
-    nh = len(hs)
-    g.scalar.dma_start(T.pt32[0:16, 0:2], T.pt[:]).then_inc(sem.s_pt, 16)
-    g.sync.dma_start(T.S[:], T.pool[:]).then_inc(sem.s_pool, 16)
+    g.iota(T.qi[:], [[0, 1]], 0, 1).then_inc(sem.k_q, 1)
     g.iota(T.mi[0:16, 0:4], [[-4, 4]], 0, 1).then_inc(sem.c_io, 1)
     g.iota(T.li[0:16, :], [[0, 8], [-1, 4], [0, 4]], 4, 1).then_inc(sem.c_io, 1)
+    v.wait_ge(sem.k_q, 1)
+    v.tensor_scalar(T.qi2[:], T.qi[:], 3, None, AluOpType.bitwise_and).then_inc(sem.k_q2, 1)
+    v.wait_ge(sem.k_q2, 1)
+    v.tensor_scalar(T.qc[:], T.qi2[:], 2.0, None, AluOpType.mult).then_inc(sem.k_qc, 1)
+    v.tensor_scalar(T.qc2[:], T.qi2[:], 2.0, 1.0, AluOpType.mult, AluOpType.add).then_inc(sem.k_qc, 1)
     v.wait_ge(sem.c_io, 2)
     v.tensor_scalar(T.mi2[0:16, :], T.mi[0:16, :], 2, None, AluOpType.arith_shift_right).then_inc(sem.c_a, 1)
     v.tensor_scalar(T.li2[0:16, :], T.li[0:16, :], 3, None, AluOpType.bitwise_and).then_inc(sem.c_a, 1)
     v.wait_ge(sem.c_a, 2)
     v.tensor_scalar(T.msk[0:16, :], T.mi2[0:16, :], 0, None, AluOpType.is_equal).then_inc(sem.c_b, 1)
     v.tensor_scalar(T.lm[0:16, :], T.li2[0:16, :], 0, None, AluOpType.is_equal).then_inc(sem.c_b, 1)
-    v.wait_ge(sem.s_pt, 16)
-    v.tensor_copy(T.ptf[0:16, :], T.pt32[0:16, :]).then_inc(sem.c_b, 1)
+    v.wait_ge(sem.k_qc, 2)
+    v.wait_ge(arrived, count)
+    v.tensor_copy(T.ptf[0:16, :], ptile[0:16, :]).then_inc(sem.c_b, 1)
     v.wait_ge(sem.c_b, 3)
     for n in range(2):
         v.tensor_scalar(T.rr[0:16, 4 * n:4 * n + 4], T.msk[0:16, :], T.ptf[0:16, n:n + 1], None,
@@ -132,99 +140,113 @@ def _rank(g, core, r, T, topo, mine, helpers):
     pe.wait_ge(sem.c_r, 2)
     pe.matmul(T.pq[:, 0:8], T.lm[0:16, :], T.rr[0:16, :], True, True).then_inc(sem.c_m, 1)
     v.wait_ge(sem.c_m, 1)
-    v.tensor_copy(T.LB[:], T.pq[:, 0:8]).then_inc(sem.c_l, 1)
-    g.wait_ge(sem.c_l, 1)
+    for b, col in enumerate((T.qc, T.qc2)):
+        v.tensor_scalar(T.OH[:, 8 * b:8 * b + 8], T.pq[:, 0:8], 8.0, col[:],
+                        AluOpType.mult, AluOpType.add).then_inc(sem.c_l, 1)
+
+
+def _rank(g, core, r, T, topo, mine, helpers):
+    sem = T.sem
+    hs = helpers[r]
+    g.vector.memset(T.pt32[:], 0).then_inc(sem.k_one, 1)
+    g.sync.wait_ge(sem.k_one, 1)
+    g.sync.dma_start(T.pt32[0:16, 0:2], T.pt[:]).then_inc(sem.s_pt, 16)
+    g.sync.dma_start(T.S[:], T.pool[:]).then_inc(sem.s_pool, 16)
     sent = 0
-    tl, td = [], []
-    for i, (h, k) in enumerate(hs):
-        m, n = _part(topo.mask(core, h), nh, i)
-        tl.append(RemoteDMATransfer(dst_ids=[_dst(topo, h)], dma_engine_mask=m, remote_sem=sem.hl,
-                                    src=T.LB[:], dst=T.HL[:]))
-        td.append(RemoteDMATransfer(dst_ids=[_dst(topo, h)], dma_engine_mask=m, remote_sem=sem.hd,
-                                    src=T.S[:, k * SW:(k + 2) * SW], dst=T.H[:]))
-        sent += 2 * n
+    tl, td = [], [[], []]
+    near = [x for x in hs if topo.die(x[0]) == topo.die(core)]
+    far = [x for x in hs if topo.die(x[0]) != topo.die(core)]
+    for lane, part in ((0, far), (1, near)):
+        for i, (h, k) in enumerate(part):
+            m, n = _lane(topo.mask(core, h), lane, len(part), i)
+            tl.append(RemoteDMATransfer(dst_ids=[_dst(topo, h)], dma_engine_mask=m, remote_sem=sem.hl,
+                                        src=T.pt32[:], dst=T.HP[:]))
+            for j in range(2):
+                td[j].append(RemoteDMATransfer(dst_ids=[_dst(topo, h)], dma_engine_mask=m, remote_sem=sem["hd%d" % j],
+                                               src=T.S[:, (k + j) * SW:(k + j + 1) * SW],
+                                               dst=T.H[:, j * SW:(j + 1) * SW]))
+            sent += 3 * n
+    g.wait_ge(sem.s_pt, 16)
     g.remote_dma_fused(tl, local_sem=sem.sent)
     g.wait_ge(sem.s_pool, 16)
-    g.remote_dma_fused(td, local_sem=sem.sent)
+    for j in range(2):
+        g.remote_dma_fused(td[j], local_sem=sem.sent)
     g.wait_ge(sem.sent, sent)
     g.sync.wait_ge(sem.yarr, sum(len(_bits(topo.mask(m, core))) for m in mine))
     g.sync.dma_start(T.y[:], T.Y[:]).then_inc(sem.done, 16)
     g.sync.wait_ge(sem.done, 16)
 
 
-def _helper(g, core, r, k, T, topo, ranks, middle, gr, nh):
+def _helper(g, core, r, k, T, topo, ranks, middle, gr, idx, na, nh):
     sem = T.sem
     v, pe = g.vector, g.tensor
     _, n_in = _part(topo.mask(ranks[r], core), nh, 0)
     _identity(g, T)
-    tl, td = [], []
-    sent = 0
+    _make_offsets(g, T, T.HP, sem.hl, n_in)
+    d = middle[gr][k + (1 if (idx + k // 2) % na == 1 else 0)]
+    rid, pid, _ = topo.addr(d)
+    m = topo.mask(core, d)
+    g.wait_ge(sem.c_l, 2)
+    g.remote_dma(T.OFF[:, r * 16:(r + 1) * 16], T.OH[:], sem["la%d" % r], sem.sent, pid, rid, m)
+    sent = len(_bits(m))
+    pe.wait_ge(sem.k_id, 1)
     for j in range(2):
-        d = middle[gr][k + j]
-        m, n = _part(topo.mask(core, d), 2, j)
-        tl.append(RemoteDMATransfer(dst_ids=[_dst(topo, d)], dma_engine_mask=m, remote_sem=sem["la%d" % r],
-                                    src=T.HL[:], dst=T.AL[:, r * 8:(r + 1) * 8]))
-        sent += n
+        pe.wait_ge(sem["hd%d" % j], n_in)
+        for b, turned in enumerate(("tf%d" % j, "tb%d" % j)):
+            ps = T["ps%d" % (NB * j + b)]
+            pe.transpose(ps[:, 0:128], T.H[:, j * SW + b * 128:j * SW + (b + 1) * 128],
+                         T.ident[:]).then_inc(sem[turned], 1)
+            v.wait_ge(sem[turned], 1)
+            v.tensor_copy(T.HT[:, j * SW + b:(j + 1) * SW:NB], ps[:, 0:128]).then_inc(sem["z%d" % j], 1)
+        td = []
         for gi in range(G):
             d = middle[gi][k + j]
-            m, n = _part(topo.mask(core, d), 2 * G, j * G + gi)
+            m, n = _part(topo.mask(core, d), G, gi)
             td.append(RemoteDMATransfer(dst_ids=[_dst(topo, d)], dma_engine_mask=m, remote_sem=sem["da%d" % r],
                                         src=T.HT[:, j * SW:(j + 1) * SW], dst=T.W[:, r * SW:(r + 1) * SW]))
             sent += n
-    g.wait_ge(sem.hl, n_in)
-    g.remote_dma_fused(tl, local_sem=sem.sent)
-    pe.wait_ge(sem.k_id, 1)
-    pe.wait_ge(sem.hd, n_in)
-    for j in range(2):
-        ps = T["ps%d" % j]
-        for b in range(NB):
-            pe.transpose(ps[:, b * 128:(b + 1) * 128], T.H[:, j * SW + b * 128:j * SW + (b + 1) * 128],
-                         T.ident[:]).then_inc(sem["tf%d" % j], 1)
-        v.wait_ge(sem["tf%d" % j], NB)
-        for b in range(NB):
-            v.tensor_copy(T.HT[:, j * SW + b:(j + 1) * SW:NB], ps[:, b * 128:(b + 1) * 128]).then_inc(sem.evv, 1)
-    g.wait_ge(sem.evv, 2 * NB)
-    g.remote_dma_fused(td, local_sem=sem.sent)
+        g.wait_ge(sem["z%d" % j], NB)
+        g.remote_dma_fused(td, local_sem=sem.sent)
     g.wait_ge(sem.sent, sent)
 
 
-def _middle(g, core, k, T, topo, ranks, askers):
+def _middle(g, core, k, T, topo, ranks, grp, partner):
     sem = T.sem
     v, sc, pe = g.vector, g.scalar, g.tensor
     off = len(_bits(topo.mask(ranks[0], core)))
-    n_list, n_data = off // 2, off // (2 * G)
-    na = len(askers)
-    askers = [askers[(k + t) % na] for t in range(na)]
+    n_data = off // G
+    na = len(grp)
+    by = {(i + k // 2) % na: r for i, r in enumerate(grp)}
+    if k % 2 == 0:
+        order, nd = [by[0], by[2], by[1]], 2
+    else:
+        order, nd = [by[1], by[0], by[2]], 1
+    direct = order[:nd]
+    n_list = {r: (off if r in direct else off // (na - nd)) for r in order}
 
-    g.iota(T.qi[:], [[0, 1]], 0, 1).then_inc(sem.k_q, 1)
     _identity(g, T)
-    v.wait_ge(sem.k_q, 1)
-    v.tensor_scalar(T.qi2[:], T.qi[:], 3, None, AluOpType.bitwise_and).then_inc(sem.k_q2, 1)
-    v.wait_ge(sem.k_q2, 1)
-    v.tensor_scalar(T.qc[:], T.qi2[:], 2.0, None, AluOpType.mult).then_inc(sem.k_qc, 1)
-    v.tensor_scalar(T.qc2[:], T.qi2[:], 2.0, 1.0, AluOpType.mult, AluOpType.add).then_inc(sem.k_qc, 1)
-    v.wait_ge(sem.k_qc, 2)
-    for r in askers:
-        v.wait_ge(sem["la%d" % r], n_list)
-        for b, col in enumerate((T.qc, T.qc2)):
-            v.tensor_scalar(T.OFF[:, r * 16 + 8 * b:r * 16 + 8 * b + 8], T.AL[:, r * 8:(r + 1) * 8], 8.0, col[:],
-                            AluOpType.mult, AluOpType.add).then_inc(sem["of%d" % r], 1)
+    tf = []
+    for i, r in enumerate(direct):
+        g.wait_ge(sem["la%d" % r], n_list[r])
+        m, n = _part(topo.mask(core, partner), nd, i)
+        tf.append(RemoteDMATransfer(dst_ids=[_dst(topo, partner)], dma_engine_mask=m, remote_sem=sem["la%d" % r],
+                                    src=T.OFF[:, r * 16:(r + 1) * 16], dst=T.OFF[:, r * 16:(r + 1) * 16]))
+    g.remote_dma_fused(tf, local_sem=sem.sent)
+    sent = off
     for q in (v, sc):
         for s in range(N):
             q.wait_ge(sem["da%d" % s], n_data)
     pe.wait_ge(sem.k_id, 1)
-    sent = 0
-    for i, r in enumerate(askers):
+    for r in order:
         ps = T["ps%d" % r]
-        win = T.W[:].indirect(T.OFF[:, r * 16:(r + 1) * 16])
-        if i == 0:
-            v.wait_ge(sem["of%d" % r], 2)
-            v.tensor_copy(T.O[:, r * SW:(r + 1) * SW], win).then_inc(sem["ga%d" % r], 1)
-        else:
-            sc.wait_ge(sem["of%d" % r], 2)
-            sc.activation(T.O[:, r * SW:(r + 1) * SW], win, ActivationFunctionType.Copy).then_inc(sem["ga%d" % r], 1)
-        pe.wait_ge(sem["ga%d" % r], 1)
-        for b in range(NB):
+        v.wait_ge(sem["la%d" % r], n_list[r])
+        v.tensor_copy(T.O[:, r * SW:r * SW + 128],
+                      T.W[:].indirect(T.OFF[:, r * 16:r * 16 + 8])).then_inc(sem["ga%d" % r], 1)
+        sc.wait_ge(sem["la%d" % r], n_list[r])
+        sc.activation(T.O[:, r * SW + 128:r * SW + 256], T.W[:].indirect(T.OFF[:, r * 16 + 8:r * 16 + 16]),
+                      ActivationFunctionType.Copy).then_inc(sem["tf%d" % r], 1)
+        for b, ready in enumerate(("ga%d" % r, "tf%d" % r)):
+            pe.wait_ge(sem[ready], 1)
             pe.transpose(ps[:, b * 128:(b + 1) * 128],
                          T.O[:, r * SW + b * 128:r * SW + (b + 1) * 128], T.ident[:]).then_inc(sem["tb%d" % r], 1)
         v.wait_ge(sem["tb%d" % r], NB)
@@ -246,10 +268,12 @@ def rank_program(g, core, T, topo):
         return
     for gi in range(G):
         if core in middle[gi]:
-            _middle(g, core, middle[gi].index(core), T, topo, ranks, groups[gi])
+            k = middle[gi].index(core)
+            _middle(g, core, k, T, topo, ranks, groups[gi], middle[gi][k + 1 - 2 * (k % 2)])
             return
     for rr, hs in helpers.items():
         for h, k in hs:
             if h == core:
-                _helper(g, core, rr, k, T, topo, ranks, middle, group_of[rr], len(hs))
+                gi = group_of[rr]
+                _helper(g, core, rr, k, T, topo, ranks, middle, gi, groups[gi].index(rr), len(groups[gi]), len(hs))
                 return

@@ -42,7 +42,7 @@ for _s in range(N):
 SEMAPHORES = ["s_pt", "s_pool", "c_io", "c_a", "c_b", "c_r", "c_m", "c_l", "sent", "yarr", "done",
               "hl", "hd0", "hd1", "k_one", "k_id", "k_q", "k_q2", "k_qc"]
 for _s in range(N):
-    SEMAPHORES += ["la%d" % _s, "da%d" % _s, "tf%d" % _s, "ga%d" % _s, "tb%d" % _s, "z%d" % _s]
+    SEMAPHORES += ["la%d" % _s, "da%d" % _s, "tf%d" % _s, "ga%d" % _s, "tb%d" % _s, "tc%d" % _s, "z%d" % _s]
 
 
 def _plan(T, topo):
@@ -52,37 +52,64 @@ def _plan(T, topo):
     for c in range(SIM_CORES):
         by_chip.setdefault(topo.chip(c), []).append(c)
 
-    def one_hop(x, rc):
-        return topo.same_plane(x, rc) or topo.mates(x, rc)
+    def hops(a, b):
+        return 0 if a == b else (1 if topo.same_plane(a, b) or topo.mates(a, b) else 2)
 
-    free = sorted([x for x in by_chip if x not in rchips],
-                  key=lambda x: (-sum(1 for rc in rchips if one_hop(x, rc)), x))
-    nch = K // 2
-    middle, dies = [], []
-    for gi in range(G):
-        per_die = {}
-        for x in free[gi * nch:(gi + 1) * nch]:
-            seen = []
-            for c in by_chip[x]:
-                if topo.die(c) not in seen and all(topo.may_write(c, r) for r in ranks):
-                    seen.append(topo.die(c))
-                    per_die.setdefault(topo.die(c), []).append(c)
-        dies = sorted(per_die, reverse=True)
-        middle.append([c for d in dies for c in per_die[d]])
-    pref = sorted(range(N), key=lambda r: (-sum(1 for x in free[:nch] if one_hop(x, rchips[r])), r))
+    narrow = topo.mask(ranks[0], ranks[1])
+    for a in ranks:
+        for b in ranks:
+            if a != b:
+                narrow &= topo.mask(a, b)
+    pref = sorted(range(N), key=lambda r: (-sum(1 for x in rchips if topo.same_plane(x, rchips[r])), r))
     groups = [sorted(pref[gi * (N // G):(gi + 1) * (N // G)]) for gi in range(G)]
+    nch = K // 2
+    used, middle, dies = [], [], []
+    for gi in range(G):
+        cand = {}
+        for x, cs in by_chip.items():
+            if x in used:
+                continue
+            per = {}
+            for c in cs:
+                if c in ranks:
+                    continue
+                if x in rchips and all(topo.may_write(c, r) for r in ranks):
+                    continue
+                if all(topo.may_write(c, ranks[a]) for a in groups[gi]):
+                    per.setdefault(topo.die(c), c)
+            if len(per) == 2:
+                cand[x] = per
+        chosen = sorted(cand, key=lambda x: (sum(1 for a in groups[gi] if hops(x, rchips[a]) == 2), x in rchips,
+                                             -sum(1 for rc in rchips if hops(x, rc) <= 1), x))[:nch]
+        used += chosen
+        dies = sorted(cand[chosen[0]], reverse=True)
+        middle.append([cand[x][d] for d in dies for x in chosen])
     every = [c for ms in middle for c in ms]
     helpers = {}
     for r, rc in enumerate(ranks):
         hs = []
         for d in dies:
             can = [c for c in by_chip[topo.chip(rc)]
-                   if c != rc and topo.die(c) == d and all(topo.may_write(c, m) for m in every)]
+                   if c != rc and c not in every and topo.die(c) == d and all(topo.may_write(c, m) for m in every)]
             first = [k for k in range(0, K, 2) if topo.die(middle[0][k]) == d]
             for j, k in enumerate(first):
                 hs.append((can[j], k))
         helpers[r] = hs
-    return ranks, middle, groups, helpers
+    turns = []
+    for gi in range(G):
+        far = [r for r in groups[gi] if any(hops(topo.chip(m), rchips[r]) == 2 for m in middle[gi])]
+        rest = [r for r in groups[gi] if r not in far]
+        per = []
+        for pair in range(K // 2):
+            if len(far) == 1:
+                d = {far[0]: 0}
+                for i, r in enumerate(rest):
+                    d[r] = 1 + (i + pair) % len(rest)
+            else:
+                d = {r: (i + pair) % len(groups[gi]) for i, r in enumerate(groups[gi])}
+            per.append(d)
+        turns.append(per)
+    return ranks, middle, groups, helpers, narrow, turns
 
 
 def _bits(mask):
@@ -148,10 +175,11 @@ def _make_offsets(g, T, ptile, arrived, count):
 def _rank(g, core, r, T, topo, mine, helpers):
     sem = T.sem
     hs = helpers[r]
-    g.vector.memset(T.pt32[:], 0).then_inc(sem.k_one, 1)
-    g.sync.wait_ge(sem.k_one, 1)
     g.sync.dma_start(T.pt32[0:16, 0:2], T.pt[:]).then_inc(sem.s_pt, 16)
+    g.scalar.dma_start(T.pt32[16:32, 0:2], T.pt[:]).then_inc(sem.s_pt, 16)
     g.sync.dma_start(T.S[:], T.pool[:]).then_inc(sem.s_pool, 16)
+    g.vector.memset(T.pt32[32:64, :], 0).then_inc(sem.k_one, 1)
+    g.vector.memset(T.pt32[64:128, :], 0).then_inc(sem.k_one, 1)
     sent = 0
     tl, td = [], [[], []]
     near = [x for x in hs if topo.die(x[0]) == topo.die(core)]
@@ -162,11 +190,13 @@ def _rank(g, core, r, T, topo, mine, helpers):
             tl.append(RemoteDMATransfer(dst_ids=[_dst(topo, h)], dma_engine_mask=m, remote_sem=sem.hl,
                                         src=T.pt32[:], dst=T.HP[:]))
             for j in range(2):
+                kk = k + (j ^ (r % 2))
                 td[j].append(RemoteDMATransfer(dst_ids=[_dst(topo, h)], dma_engine_mask=m, remote_sem=sem["hd%d" % j],
-                                               src=T.S[:, (k + j) * SW:(k + j + 1) * SW],
+                                               src=T.S[:, kk * SW:(kk + 1) * SW],
                                                dst=T.H[:, j * SW:(j + 1) * SW]))
             sent += 3 * n
-    g.wait_ge(sem.s_pt, 16)
+    g.wait_ge(sem.k_one, 2)
+    g.wait_ge(sem.s_pt, 32)
     g.remote_dma_fused(tl, local_sem=sem.sent)
     g.wait_ge(sem.s_pool, 16)
     for j in range(2):
@@ -177,20 +207,28 @@ def _rank(g, core, r, T, topo, mine, helpers):
     g.sync.wait_ge(sem.done, 16)
 
 
-def _helper(g, core, r, k, T, topo, ranks, middle, gr, idx, na, nh):
+def _helper(g, core, r, k, T, topo, ranks, middle, gr, turn, nh, narrow):
     sem = T.sem
     v, pe = g.vector, g.tensor
     _, n_in = _part(topo.mask(ranks[r], core), nh, 0)
     _identity(g, T)
     _make_offsets(g, T, T.HP, sem.hl, n_in)
-    d = middle[gr][k + (1 if (idx + k // 2) % na == 1 else 0)]
-    rid, pid, _ = topo.addr(d)
-    m = topo.mask(core, d)
+    to = {0: [middle[gr][k], middle[gr][k + 1]], 1: [middle[gr][k + 1]], 2: [middle[gr][k]]}[turn]
+    both = narrow
+    for d in to:
+        both &= topo.mask(core, d)
+    tl = []
+    sent = 0
+    for i, d in enumerate(to):
+        m, n = _part(both, len(to), i)
+        tl.append(RemoteDMATransfer(dst_ids=[_dst(topo, d)], dma_engine_mask=m, remote_sem=sem["la%d" % r],
+                                    src=T.OH[:], dst=T.OFF[:, r * 16:(r + 1) * 16]))
+        sent += n
     g.wait_ge(sem.c_l, 2)
-    g.remote_dma(T.OFF[:, r * 16:(r + 1) * 16], T.OH[:], sem["la%d" % r], sem.sent, pid, rid, m)
-    sent = len(_bits(m))
+    g.remote_dma_fused(tl, local_sem=sem.sent)
     pe.wait_ge(sem.k_id, 1)
     for j in range(2):
+        kk = k + (j ^ (r % 2))
         pe.wait_ge(sem["hd%d" % j], n_in)
         for b, turned in enumerate(("tf%d" % j, "tb%d" % j)):
             ps = T["ps%d" % (NB * j + b)]
@@ -198,11 +236,14 @@ def _helper(g, core, r, k, T, topo, ranks, middle, gr, idx, na, nh):
                          T.ident[:]).then_inc(sem[turned], 1)
             v.wait_ge(sem[turned], 1)
             v.tensor_copy(T.HT[:, j * SW + b:(j + 1) * SW:NB], ps[:, 0:128]).then_inc(sem["z%d" % j], 1)
+        both = narrow
+        for gi in range(G):
+            both &= topo.mask(core, middle[gi][kk])
         td = []
         for gi in range(G):
-            d = middle[gi][k + j]
-            m, n = _part(topo.mask(core, d), G, gi)
-            td.append(RemoteDMATransfer(dst_ids=[_dst(topo, d)], dma_engine_mask=m, remote_sem=sem["da%d" % r],
+            m, n = _part(both, G, gi)
+            td.append(RemoteDMATransfer(dst_ids=[_dst(topo, middle[gi][kk])], dma_engine_mask=m,
+                                        remote_sem=sem["da%d" % r],
                                         src=T.HT[:, j * SW:(j + 1) * SW], dst=T.W[:, r * SW:(r + 1) * SW]))
             sent += n
         g.wait_ge(sem["z%d" % j], NB)
@@ -210,57 +251,53 @@ def _helper(g, core, r, k, T, topo, ranks, middle, gr, idx, na, nh):
     g.wait_ge(sem.sent, sent)
 
 
-def _middle(g, core, k, T, topo, ranks, grp, partner):
+def _middle(g, core, k, T, topo, ranks, turn, partner, narrow):
     sem = T.sem
     v, sc, pe = g.vector, g.scalar, g.tensor
-    off = len(_bits(topo.mask(ranks[0], core)))
+    off = len(_bits(narrow))
     n_data = off // G
-    na = len(grp)
-    by = {(i + k // 2) % na: r for i, r in enumerate(grp)}
+    by = {t: r for r, t in turn.items()}
     if k % 2 == 0:
-        order, nd = [by[0], by[2], by[1]], 2
+        order, pas = [by[0], by[2], by[1]], by[2]
     else:
-        order, nd = [by[1], by[0], by[2]], 1
-    direct = order[:nd]
-    n_list = {r: (off if r in direct else off // (na - nd)) for r in order}
+        order, pas = [by[1], by[0], by[2]], by[1]
+    n_list = {r: (off // 2 if r == by[0] else off) for r in order}
 
     _identity(g, T)
-    tf = []
-    for i, r in enumerate(direct):
-        g.wait_ge(sem["la%d" % r], n_list[r])
-        m, n = _part(topo.mask(core, partner), nd, i)
-        tf.append(RemoteDMATransfer(dst_ids=[_dst(topo, partner)], dma_engine_mask=m, remote_sem=sem["la%d" % r],
-                                    src=T.OFF[:, r * 16:(r + 1) * 16], dst=T.OFF[:, r * 16:(r + 1) * 16]))
-    g.remote_dma_fused(tf, local_sem=sem.sent)
-    sent = off
+    rid, pid, _ = topo.addr(partner)
+    m = topo.mask(core, partner) & narrow
+    g.wait_ge(sem["la%d" % pas], n_list[pas])
+    g.remote_dma(T.OFF[:, pas * 16:(pas + 1) * 16], T.OFF[:, pas * 16:(pas + 1) * 16], sem["la%d" % pas], sem.sent,
+                 pid, rid, m)
+    sent = len(_bits(m))
     for q in (v, sc):
         for s in range(N):
             q.wait_ge(sem["da%d" % s], n_data)
     pe.wait_ge(sem.k_id, 1)
-    for r in order:
-        ps = T["ps%d" % r]
+    for pos, r in enumerate(order):
         v.wait_ge(sem["la%d" % r], n_list[r])
         v.tensor_copy(T.O[:, r * SW:r * SW + 128],
                       T.W[:].indirect(T.OFF[:, r * 16:r * 16 + 8])).then_inc(sem["ga%d" % r], 1)
         sc.wait_ge(sem["la%d" % r], n_list[r])
         sc.activation(T.O[:, r * SW + 128:r * SW + 256], T.W[:].indirect(T.OFF[:, r * 16 + 8:r * 16 + 16]),
                       ActivationFunctionType.Copy).then_inc(sem["tf%d" % r], 1)
-        for b, ready in enumerate(("ga%d" % r, "tf%d" % r)):
+        for b, (ready, turned) in enumerate((("ga%d" % r, "tb%d" % r), ("tf%d" % r, "tc%d" % r))):
+            ps = T["ps%d" % (NB * pos + b)]
             pe.wait_ge(sem[ready], 1)
-            pe.transpose(ps[:, b * 128:(b + 1) * 128],
-                         T.O[:, r * SW + b * 128:r * SW + (b + 1) * 128], T.ident[:]).then_inc(sem["tb%d" % r], 1)
-        v.wait_ge(sem["tb%d" % r], NB)
-        v.tensor_copy(T.Z[:, r * SW:(r + 1) * SW], ps[:, 0:SW]).then_inc(sem["z%d" % r], 1)
+            pe.transpose(ps[:, 0:128],
+                         T.O[:, r * SW + b * 128:r * SW + (b + 1) * 128], T.ident[:]).then_inc(sem[turned], 1)
+            v.wait_ge(sem[turned], 1)
+            v.tensor_copy(T.Z[:, r * SW + b * 128:r * SW + (b + 1) * 128], ps[:, 0:128]).then_inc(sem["z%d" % r], 1)
         rid, pid, _ = topo.addr(ranks[r])
         m = topo.mask(core, ranks[r])
-        g.wait_ge(sem["z%d" % r], 1)
+        g.wait_ge(sem["z%d" % r], NB)
         g.remote_dma(T.Y[:, k * SW:(k + 1) * SW], T.Z[:, r * SW:(r + 1) * SW], sem.yarr, sem.sent, pid, rid, m)
         sent += len(_bits(m))
     g.wait_ge(sem.sent, sent)
 
 
 def rank_program(g, core, T, topo):
-    ranks, middle, groups, helpers = _plan(T, topo)
+    ranks, middle, groups, helpers, narrow, turns = _plan(T, topo)
     group_of = {r: gi for gi, rs in enumerate(groups) for r in rs}
     r = T.rank_of(core)
     if r is not None:
@@ -269,11 +306,11 @@ def rank_program(g, core, T, topo):
     for gi in range(G):
         if core in middle[gi]:
             k = middle[gi].index(core)
-            _middle(g, core, k, T, topo, ranks, groups[gi], middle[gi][k + 1 - 2 * (k % 2)])
+            _middle(g, core, k, T, topo, ranks, turns[gi][k // 2], middle[gi][k + 1 - 2 * (k % 2)], narrow)
             return
     for rr, hs in helpers.items():
         for h, k in hs:
             if h == core:
                 gi = group_of[rr]
-                _helper(g, core, rr, k, T, topo, ranks, middle, gi, groups[gi].index(rr), len(groups[gi]), len(hs))
+                _helper(g, core, rr, k, T, topo, ranks, middle, gi, turns[gi][k // 2][rr], len(hs), narrow)
                 return

from concourse.bass import DstId, RemoteDMATransfer
from concourse.mybir import AluOpType, ActivationFunctionType

N = 6
K = 8
G = 2
SW = 2048 // K
NB = SW // 128
SIM_CORES = 112

SCRATCH = {
    "S": ("sbuf", [128, 2048], "bfloat16"),
    "Y": ("sbuf", [128, 2048], "bfloat16"),
    "pt32": ("sbuf", [128, 2], "int32"),
    "HP": ("sbuf", [128, 2], "int32"),
    "ptf": ("sbuf", [128, 2], "float32"),
    "mi": ("sbuf", [128, 4], "int32"),
    "mi2": ("sbuf", [128, 4], "int32"),
    "msk": ("sbuf", [128, 4], "float32"),
    "li": ("sbuf", [128, 128], "int32"),
    "li2": ("sbuf", [128, 128], "int32"),
    "lm": ("sbuf", [128, 128], "bfloat16"),
    "rr": ("sbuf", [128, 8], "bfloat16"),
    "qi": ("sbuf", [128, 1], "int32"),
    "qi2": ("sbuf", [128, 1], "int32"),
    "qc": ("sbuf", [128, 1], "float32"),
    "qc2": ("sbuf", [128, 1], "float32"),
    "OH": ("sbuf", [128, 16], "uint16"),
    "pq": ("psum", [128, 512], "float32"),
    "H": ("sbuf", [128, 2 * SW], "bfloat16"),
    "HT": ("sbuf", [128, 2 * SW], "bfloat16"),
    "ones": ("sbuf", [128, 128], "bfloat16"),
    "ident": ("sbuf", [128, 128], "bfloat16"),
    "OFF": ("sbuf", [128, N * 16], "uint16"),
    "W": ("sbuf", [128, N * SW], "bfloat16"),
    "O": ("sbuf", [128, N * SW], "bfloat16"),
    "Z": ("sbuf", [128, N * SW], "bfloat16"),
}
for _s in range(N):
    SCRATCH["ps%d" % _s] = ("psum", [128, 1024], "bfloat16")

SEMAPHORES = ["s_pt", "s_pool", "c_io", "c_a", "c_b", "c_r", "c_m", "c_l", "sent", "yarr", "done",
              "hl", "hd0", "hd1", "k_one", "k_id", "k_q", "k_q2", "k_qc"]
for _s in range(N):
    SEMAPHORES += ["la%d" % _s, "da%d" % _s, "tf%d" % _s, "ga%d" % _s, "tb%d" % _s, "tc%d" % _s, "z%d" % _s]


def _plan(T, topo):
    ranks = list(T.cores)
    rchips = [topo.chip(c) for c in ranks]
    by_chip = {}
    for c in range(SIM_CORES):
        by_chip.setdefault(topo.chip(c), []).append(c)

    def hops(a, b):
        return 0 if a == b else (1 if topo.same_plane(a, b) or topo.mates(a, b) else 2)

    narrow = topo.mask(ranks[0], ranks[1])
    for a in ranks:
        for b in ranks:
            if a != b:
                narrow &= topo.mask(a, b)
    pref = sorted(range(N), key=lambda r: (-sum(1 for x in rchips if topo.same_plane(x, rchips[r])), r))
    groups = [sorted(pref[gi * (N // G):(gi + 1) * (N // G)]) for gi in range(G)]
    nch = K // 2
    used, middle, dies = [], [], []
    for gi in range(G):
        cand = {}
        for x, cs in by_chip.items():
            if x in used:
                continue
            per = {}
            for c in cs:
                if c in ranks:
                    continue
                if x in rchips and all(topo.may_write(c, r) for r in ranks):
                    continue
                if all(topo.may_write(c, ranks[a]) for a in groups[gi]):
                    per.setdefault(topo.die(c), c)
            if len(per) == 2:
                cand[x] = per
        chosen = sorted(cand, key=lambda x: (sum(1 for a in groups[gi] if hops(x, rchips[a]) == 2), x in rchips,
                                             -sum(1 for rc in rchips if hops(x, rc) <= 1), x))[:nch]
        used += chosen
        dies = sorted(cand[chosen[0]], reverse=True)
        middle.append([cand[x][d] for d in dies for x in chosen])
    every = [c for ms in middle for c in ms]
    helpers = {}
    for r, rc in enumerate(ranks):
        hs = []
        for d in dies:
            can = [c for c in by_chip[topo.chip(rc)]
                   if c != rc and c not in every and topo.die(c) == d and all(topo.may_write(c, m) for m in every)]
            first = [k for k in range(0, K, 2) if topo.die(middle[0][k]) == d]
            for j, k in enumerate(first):
                hs.append((can[j], k))
        helpers[r] = hs
    turns = []
    for gi in range(G):
        far = [r for r in groups[gi] if any(hops(topo.chip(m), rchips[r]) == 2 for m in middle[gi])]
        rest = [r for r in groups[gi] if r not in far]
        per = []
        for pair in range(K // 2):
            if len(far) == 1:
                d = {far[0]: 0}
                for i, r in enumerate(rest):
                    d[r] = 1 + (i + pair) % len(rest)
            else:
                d = {r: (i + pair) % len(groups[gi]) for i, r in enumerate(groups[gi])}
            per.append(d)
        turns.append(per)
    return ranks, middle, groups, helpers, narrow, turns


def _bits(mask):
    return [b for b in range(16) if (mask >> b) & 1]


def _part(mask, parts, i):
    b = _bits(mask)
    n = len(b) // parts
    return sum(1 << e for e in b[i * n:(i + 1) * n]), n


def _lane(mask, lane, parts, i):
    b = _bits(mask)[lane::2]
    n = len(b) // parts
    return sum(1 << e for e in b[i * n:(i + 1) * n]), n


def _dst(topo, c):
    rid, pid, _ = topo.addr(c)
    return DstId(rid=rid, pnc=pid)


def _identity(g, T):
    g.vector.memset(T.ones[:], 1.0).then_inc(T.sem.k_one, 1)
    g.wait_ge(T.sem.k_one, 1)
    g.affine_select(T.ident[:], T.ones[:], [[-1, 128]], AluOpType.is_equal, 0.0, 0, 1).then_inc(T.sem.k_id, 1)


def _make_offsets(g, T, ptile, arrived, count):
    sem = T.sem
    v, pe = g.vector, g.tensor
    g.iota(T.qi[:], [[0, 1]], 0, 1).then_inc(sem.k_q, 1)
    g.iota(T.mi[0:16, 0:4], [[-4, 4]], 0, 1).then_inc(sem.c_io, 1)
    g.iota(T.li[0:16, :], [[0, 8], [-1, 4], [0, 4]], 4, 1).then_inc(sem.c_io, 1)
    v.wait_ge(sem.k_q, 1)
    v.tensor_scalar(T.qi2[:], T.qi[:], 3, None, AluOpType.bitwise_and).then_inc(sem.k_q2, 1)
    v.wait_ge(sem.k_q2, 1)
    v.tensor_scalar(T.qc[:], T.qi2[:], 2.0, None, AluOpType.mult).then_inc(sem.k_qc, 1)
    v.tensor_scalar(T.qc2[:], T.qi2[:], 2.0, 1.0, AluOpType.mult, AluOpType.add).then_inc(sem.k_qc, 1)
    v.wait_ge(sem.c_io, 2)
    v.tensor_scalar(T.mi2[0:16, :], T.mi[0:16, :], 2, None, AluOpType.arith_shift_right).then_inc(sem.c_a, 1)
    v.tensor_scalar(T.li2[0:16, :], T.li[0:16, :], 3, None, AluOpType.bitwise_and).then_inc(sem.c_a, 1)
    v.wait_ge(sem.c_a, 2)
    v.tensor_scalar(T.msk[0:16, :], T.mi2[0:16, :], 0, None, AluOpType.is_equal).then_inc(sem.c_b, 1)
    v.tensor_scalar(T.lm[0:16, :], T.li2[0:16, :], 0, None, AluOpType.is_equal).then_inc(sem.c_b, 1)
    v.wait_ge(sem.k_qc, 2)
    v.wait_ge(arrived, count)
    v.tensor_copy(T.ptf[0:16, :], ptile[0:16, :]).then_inc(sem.c_b, 1)
    v.wait_ge(sem.c_b, 3)
    for n in range(2):
        v.tensor_scalar(T.rr[0:16, 4 * n:4 * n + 4], T.msk[0:16, :], T.ptf[0:16, n:n + 1], None,
                        AluOpType.mult).then_inc(sem.c_r, 1)
    pe.wait_ge(sem.c_b, 3)
    pe.wait_ge(sem.c_r, 2)
    pe.matmul(T.pq[:, 0:8], T.lm[0:16, :], T.rr[0:16, :], True, True).then_inc(sem.c_m, 1)
    v.wait_ge(sem.c_m, 1)
    for b, col in enumerate((T.qc, T.qc2)):
        v.tensor_scalar(T.OH[:, 8 * b:8 * b + 8], T.pq[:, 0:8], 8.0, col[:],
                        AluOpType.mult, AluOpType.add).then_inc(sem.c_l, 1)


def _rank(g, core, r, T, topo, mine, helpers):
    sem = T.sem
    hs = helpers[r]
    g.sync.dma_start(T.pt32[0:16, 0:2], T.pt[:]).then_inc(sem.s_pt, 16)
    g.scalar.dma_start(T.pt32[16:32, 0:2], T.pt[:]).then_inc(sem.s_pt, 16)
    g.sync.dma_start(T.S[:], T.pool[:]).then_inc(sem.s_pool, 16)
    g.vector.memset(T.pt32[32:64, :], 0).then_inc(sem.k_one, 1)
    g.vector.memset(T.pt32[64:128, :], 0).then_inc(sem.k_one, 1)
    sent = 0
    tl, td = [], [[], []]
    near = [x for x in hs if topo.die(x[0]) == topo.die(core)]
    far = [x for x in hs if topo.die(x[0]) != topo.die(core)]
    for lane, part in ((0, far), (1, near)):
        for i, (h, k) in enumerate(part):
            m, n = _lane(topo.mask(core, h), lane, len(part), i)
            tl.append(RemoteDMATransfer(dst_ids=[_dst(topo, h)], dma_engine_mask=m, remote_sem=sem.hl,
                                        src=T.pt32[:], dst=T.HP[:]))
            for j in range(2):
                kk = k + (j ^ (r % 2))
                td[j].append(RemoteDMATransfer(dst_ids=[_dst(topo, h)], dma_engine_mask=m, remote_sem=sem["hd%d" % j],
                                               src=T.S[:, kk * SW:(kk + 1) * SW],
                                               dst=T.H[:, j * SW:(j + 1) * SW]))
            sent += 3 * n
    g.wait_ge(sem.k_one, 2)
    g.wait_ge(sem.s_pt, 32)
    g.remote_dma_fused(tl, local_sem=sem.sent)
    g.wait_ge(sem.s_pool, 16)
    for j in range(2):
        g.remote_dma_fused(td[j], local_sem=sem.sent)
    g.wait_ge(sem.sent, sent)
    g.sync.wait_ge(sem.yarr, sum(len(_bits(topo.mask(m, core))) for m in mine))
    g.sync.dma_start(T.y[:], T.Y[:]).then_inc(sem.done, 16)
    g.sync.wait_ge(sem.done, 16)


def _helper(g, core, r, k, T, topo, ranks, middle, gr, turn, nh, narrow):
    sem = T.sem
    v, pe = g.vector, g.tensor
    _, n_in = _part(topo.mask(ranks[r], core), nh, 0)
    _identity(g, T)
    _make_offsets(g, T, T.HP, sem.hl, n_in)
    to = {0: [middle[gr][k], middle[gr][k + 1]], 1: [middle[gr][k + 1]], 2: [middle[gr][k]]}[turn]
    both = narrow
    for d in to:
        both &= topo.mask(core, d)
    tl = []
    sent = 0
    for i, d in enumerate(to):
        m, n = _part(both, len(to), i)
        tl.append(RemoteDMATransfer(dst_ids=[_dst(topo, d)], dma_engine_mask=m, remote_sem=sem["la%d" % r],
                                    src=T.OH[:], dst=T.OFF[:, r * 16:(r + 1) * 16]))
        sent += n
    g.wait_ge(sem.c_l, 2)
    g.remote_dma_fused(tl, local_sem=sem.sent)
    pe.wait_ge(sem.k_id, 1)
    for j in range(2):
        kk = k + (j ^ (r % 2))
        pe.wait_ge(sem["hd%d" % j], n_in)
        for b, turned in enumerate(("tf%d" % j, "tb%d" % j)):
            ps = T["ps%d" % (NB * j + b)]
            pe.transpose(ps[:, 0:128], T.H[:, j * SW + b * 128:j * SW + (b + 1) * 128],
                         T.ident[:]).then_inc(sem[turned], 1)
            v.wait_ge(sem[turned], 1)
            v.tensor_copy(T.HT[:, j * SW + b:(j + 1) * SW:NB], ps[:, 0:128]).then_inc(sem["z%d" % j], 1)
        both = narrow
        for gi in range(G):
            both &= topo.mask(core, middle[gi][kk])
        td = []
        for gi in range(G):
            m, n = _part(both, G, gi)
            td.append(RemoteDMATransfer(dst_ids=[_dst(topo, middle[gi][kk])], dma_engine_mask=m,
                                        remote_sem=sem["da%d" % r],
                                        src=T.HT[:, j * SW:(j + 1) * SW], dst=T.W[:, r * SW:(r + 1) * SW]))
            sent += n
        g.wait_ge(sem["z%d" % j], NB)
        g.remote_dma_fused(td, local_sem=sem.sent)
    g.wait_ge(sem.sent, sent)


def _middle(g, core, k, T, topo, ranks, turn, partner, narrow):
    sem = T.sem
    v, sc, pe = g.vector, g.scalar, g.tensor
    off = len(_bits(narrow))
    n_data = off // G
    by = {t: r for r, t in turn.items()}
    if k % 2 == 0:
        order, pas = [by[0], by[2], by[1]], by[2]
    else:
        order, pas = [by[1], by[0], by[2]], by[1]
    n_list = {r: (off // 2 if r == by[0] else off) for r in order}

    _identity(g, T)
    rid, pid, _ = topo.addr(partner)
    m = topo.mask(core, partner) & narrow
    g.wait_ge(sem["la%d" % pas], n_list[pas])
    g.remote_dma(T.OFF[:, pas * 16:(pas + 1) * 16], T.OFF[:, pas * 16:(pas + 1) * 16], sem["la%d" % pas], sem.sent,
                 pid, rid, m)
    sent = len(_bits(m))
    for q in (v, sc):
        for s in range(N):
            q.wait_ge(sem["da%d" % s], n_data)
    pe.wait_ge(sem.k_id, 1)
    for pos, r in enumerate(order):
        v.wait_ge(sem["la%d" % r], n_list[r])
        v.tensor_copy(T.O[:, r * SW:r * SW + 128],
                      T.W[:].indirect(T.OFF[:, r * 16:r * 16 + 8])).then_inc(sem["ga%d" % r], 1)
        sc.wait_ge(sem["la%d" % r], n_list[r])
        sc.activation(T.O[:, r * SW + 128:r * SW + 256], T.W[:].indirect(T.OFF[:, r * 16 + 8:r * 16 + 16]),
                      ActivationFunctionType.Copy).then_inc(sem["tf%d" % r], 1)
        for b, (ready, turned) in enumerate((("ga%d" % r, "tb%d" % r), ("tf%d" % r, "tc%d" % r))):
            ps = T["ps%d" % (NB * pos + b)]
            pe.wait_ge(sem[ready], 1)
            pe.transpose(ps[:, 0:128],
                         T.O[:, r * SW + b * 128:r * SW + (b + 1) * 128], T.ident[:]).then_inc(sem[turned], 1)
            v.wait_ge(sem[turned], 1)
            v.tensor_copy(T.Z[:, r * SW + b * 128:r * SW + (b + 1) * 128], ps[:, 0:128]).then_inc(sem["z%d" % r], 1)
        rid, pid, _ = topo.addr(ranks[r])
        m = topo.mask(core, ranks[r])
        g.wait_ge(sem["z%d" % r], NB)
        g.remote_dma(T.Y[:, k * SW:(k + 1) * SW], T.Z[:, r * SW:(r + 1) * SW], sem.yarr, sem.sent, pid, rid, m)
        sent += len(_bits(m))
    g.wait_ge(sem.sent, sent)


def rank_program(g, core, T, topo):
    ranks, middle, groups, helpers, narrow, turns = _plan(T, topo)
    group_of = {r: gi for gi, rs in enumerate(groups) for r in rs}
    r = T.rank_of(core)
    if r is not None:
        _rank(g, core, r, T, topo, middle[group_of[r]], helpers)
        return
    for gi in range(G):
        if core in middle[gi]:
            k = middle[gi].index(core)
            _middle(g, core, k, T, topo, ranks, turns[gi][k // 2], middle[gi][k + 1 - 2 * (k % 2)], narrow)
            return
    for rr, hs in helpers.items():
        for h, k in hs:
            if h == core:
                gi = group_of[rr]
                _helper(g, core, rr, k, T, topo, ranks, middle, gi, turns[gi][k // 2][rr], len(hs), narrow)
                return
